import numpy as np
import ml_dtypes


def mxq(x, axis, fmt="e4m3"):
    dtype, down = {"e4m3": (ml_dtypes.float8_e4m3fn, 7), "e5m2": (ml_dtypes.float8_e5m2, 14)}[fmt]
    v = np.moveaxis(np.asarray(x, np.float32).astype(ml_dtypes.bfloat16).astype(np.float64), axis, -1)
    blocks = v.reshape(v.shape[:-1] + (-1, 32))
    amax = np.abs(blocks).max(-1, keepdims=True)
    byte = np.maximum(np.where(amax > 0, np.frexp(amax)[1] - 1 + 127, 0) - down, 1)
    scale = np.exp2(byte - 127.0)
    codes = (blocks / scale).astype(np.float32).astype(dtype).astype(np.float64)
    return np.moveaxis((codes * scale).reshape(v.shape), -1, axis)


WIDE = False


def mx_kscale(k):
    if not WIDE:
        return np.ones(k)
    levels = np.array([10, -10, 5, -5, 0])
    if k % 512:
        return np.exp2(np.random.permutation(np.resize(levels, k // 32))).repeat(32)
    a = np.empty((k // 512, 16))
    for p in range(k // 512):
        a[p, :8] = np.random.permutation(np.resize(levels, 8))
        for g in range(8):
            far = levels[np.abs(levels - a[p, g]) >= 10]
            a[p, g + 8] = far[np.random.randint(len(far))]
    return np.exp2(a.ravel()).repeat(32)


def f64(x):
    return np.asarray(x).astype(np.float64)


def striped(idx):
    return np.tile(idx.reshape(-1, 16).T, (8, 1)).astype(np.uint16)


def unstriped(offs):
    return offs[:16].T.reshape(-1).astype(np.int64)


def pack_weight(w):
    k, n = w.shape
    w = f64(np.asarray(w, np.float32).astype(ml_dtypes.bfloat16)).reshape(k // 32, 32, n)
    amax = np.abs(w).max(1)
    byte = np.clip(np.where(amax > 0, np.frexp(amax)[1] - 1 + 127 - 7, 1), 1, 254)
    scaled = (w * np.exp2(127.0 - byte)[:, None, :]).reshape(k, n).astype(np.float32)
    words = np.ascontiguousarray(scaled.reshape(k // 512, 128, 4, n).transpose(0, 1, 3, 2)).astype(ml_dtypes.float8_e4m3fn).view(np.uint8)
    return words, np.ascontiguousarray(byte.astype(np.uint8).reshape(k // 512, 16, n))


def unpack_weight(words, scales):
    g, p, n, _ = words.shape
    vals = np.ascontiguousarray(words).view(ml_dtypes.float8_e4m3fn).astype(np.float64) * np.repeat(np.exp2(scales.astype(np.float64) - 127.0), 8, axis=1)[..., None]
    return vals.transpose(0, 1, 3, 2).reshape(g * 512, n)


def relu(v):
    return np.maximum(v, 0.0)


K, T, D, S, V, N = 1536, 2048, 16, 1024, 64, 128


def setup_inputs():
    n = np.random.standard_normal
    s = mx_kscale(K)[:, None]
    words, scales = pack_weight(n((K, N)) / np.sqrt(K) / s)
    return {
        "xT": (n((K, T)) * s).astype(np.float32),
        "w_words": words,
        "w_scales": scales,
        "b": (0.3 * n((N, 1))).astype(np.float32),
        "offs": striped(np.random.permutation(T)[:S]),
    }


def reference(xT, w_words, w_scales, b, offs):
    w = unpack_weight(w_words, w_scales)
    idx = unstriped(offs)
    xq = mxq(f64(xT)[:, idx], 0, "e4m3")
    y = w.T @ xq
    y = relu(y + f64(b))
    return y.reshape(N, V, D).max(axis=2)

@@ -1,0 +1,110 @@
+import concourse.mybir as mybir
+
+K, T, D, S, V, N = 1536, 2048, 16, 1024, 64, 128
+FLOPS = 2 * K * S * N
+
+F32 = mybir.dt.float32
+BF16 = mybir.dt.bfloat16
+I32 = mybir.dt.int32
+U32 = mybir.dt.uint32
+U16 = mybir.dt.uint16
+U8 = mybir.dt.uint8
+FP8X4 = mybir.dt.float8_e4m3fn_x4
+Copy = mybir.ActivationFunctionType.Copy
+Op = mybir.AluOpType
+
+P = 128
+PASSES = K // 512
+HALF = S // 2
+BODY_LOADS = [(0, 1024), (1024, 2048)]
+BODY_CASTS = [(0, 1024, "s"), (1024, 1536, "s"), (1536, 2048, "v")]
+LAST_LOADS = [(0, 512), (512, 1024), (1024, 1536), (1536, 1792), (1792, 2048)]
+LAST_CASTS = [(0, 512, "s"), (512, 1024, "s"), (1024, 1536, "v"), (1536, 1792, "s"), (1792, 2048, "v")]
+
+
+def tile_picked_pool_lin_relu_sub_e_kernel(tc, xT, w_words, w_scales, b, offs, out):
+    nc = tc.nc
+    with tc.tile_pool(name="keep", bufs=1) as keep, tc.psum_pool(name="psum", bufs=1) as psum:
+        offsets = keep.tile([P, S // 16], U16, name="offsets")
+        w_codes = keep.tile([P, PASSES, N * 4], U8, name="w_codes", align_bytes=64)
+        w_planes = keep.tile([P, PASSES, N], U8, name="w_planes", align_bytes=64)
+        bias = keep.tile([P, 1], F32, name="bias")
+        raw = [keep.tile([P, 2, T], F32, name=f"raw{i}") for i in range(2 * PASSES)]
+        pairs = [keep.tile([P, T, 2], BF16, name=f"pairs{i}", align_bytes=64) for i in range(2 * PASSES)]
+        grouped = [keep.tile([P, S, 4], BF16, name=f"grouped{a}", align_bytes=64) for a in range(PASSES)]
+        codes = [keep.tile([P, S], U32, name=f"codes{a}", align_bytes=64) for a in range(PASSES)]
+        planes = [keep.tile([P, S], U8, name=f"planes{a}", align_bytes=64) for a in range(PASSES)]
+        largest = keep.tile([P, V], F32, name="largest")
+        result = keep.tile([P, V], F32, name="result")
+        acc = [psum.tile([P, HALF], F32, name=f"acc{h}") for h in range(2)]
+
+        def loads(i):
+            return LAST_LOADS if i == 2 * PASSES - 1 else BODY_LOADS
+
+        def casts(i):
+            return LAST_CASTS if i == 2 * PASSES - 1 else BODY_CASTS
+
+        nc.vector.memset(w_planes[:].rearrange("p a n -> p (a n)").bitcast(I32), 0)
+        for i in range(2 * PASSES):
+            a, u = divmod(i, 2)
+            rows = xT[512 * a : 512 * (a + 1), :].rearrange("(p j) t -> p j t", j=4)
+            for t0, t1 in loads(i):
+                nc.sync.dma_start(out=raw[i][:, :, t0:t1], in_=rows[:, 2 * u : 2 * u + 2, t0:t1])
+            if i == 0:
+                nc.sync.dma_start(offsets[:], offs)
+                nc.scalar.dma_start(out=w_codes[:].bitcast(I32), in_=w_words.rearrange("a p m r -> p a (m r)").bitcast(I32))
+                for q in range(4):
+                    nc.scalar.dma_start(
+                        out=w_planes[32 * q : 32 * q + 4, :, :].bitcast(I32),
+                        in_=w_scales[:, 4 * q : 4 * q + 4, :].rearrange("a q m -> q a m").bitcast(I32),
+                    )
+                nc.scalar.dma_start(out=bias[:], in_=b)
+
+        def gather(i, c0, c1):
+            a, u = divmod(i, 2)
+            words = grouped[a][:].rearrange("p n j -> p (n j)").bitcast(U32).rearrange("p (n u) -> p n u", u=2)
+            window = pairs[i][:].rearrange("p t e -> p (t e)").bitcast(U32)
+            nc.vector.tensor_copy(out=words[:, c0:c1, u], in_=window.indirect(offsets[:, c0 // 16 : c1 // 16]))
+
+        def quantize(a, c0, c1):
+            nc.vector.quantize_mx(
+                out=codes[a][:, c0:c1].bitcast(FP8X4),
+                scales=planes[a][:, c0:c1],
+                in_=grouped[a][:].rearrange("p n j -> p (n j)")[:, 4 * c0 : 4 * c1],
+            )
+
+        for i in range(2 * PASSES):
+            a, u = divmod(i, 2)
+            for t0, t1, engine in casts(i):
+                src = raw[i][:, :, t0:t1].rearrange("p e t -> p t e")
+                if engine == "s":
+                    nc.scalar.activation(pairs[i][:, t0:t1, :], src, Copy)
+                else:
+                    nc.vector.tensor_copy(out=pairs[i][:, t0:t1, :], in_=src)
+            if u == 0:
+                gather(i, 0, S)
+                continue
+            for h in range(2):
+                gather(i, h * HALF, (h + 1) * HALF)
+            for h in range(2):
+                quantize(a, h * HALF, (h + 1) * HALF)
+            for h in range(2):
+                cols = slice(h * HALF, (h + 1) * HALF)
+                nc.tensor.matmul_mx(
+                    out=acc[h][:],
+                    lhsT=w_codes[:, a, :].bitcast(FP8X4),
+                    lhsT_scale=w_planes[:, a, :],
+                    rhs=codes[a][:, cols].bitcast(FP8X4),
+                    rhs_scale=planes[a][:, cols],
+                    start=(a == 0),
+                    stop=(a == PASSES - 1),
+                )
+        for h in range(2):
+            nc.vector.tensor_reduce(
+                out=largest[:, h * V // 2 : (h + 1) * V // 2],
+                in_=acc[h][:].rearrange("p (v d) -> p v d", d=D),
+                axis=mybir.AxisListType.X,
+                op=Op.max,
+            )
+        nc.vector.tensor_scalar(out=result[:], in0=largest[:], scalar1=bias[:, 0:1], scalar2=0.0, op0=Op.add, op1=Op.max)
+        nc.sync.dma_start(out=out, in_=result[:])

@@ -16,10 +16,17 @@ Op = mybir.AluOpType
 P = 128
 PASSES = K // 512
 HALF = S // 2
-BODY_LOADS = [(0, 1024), (1024, 2048)]
-BODY_CASTS = [(0, 1024, "s"), (1024, 1536, "s"), (1536, 2048, "v")]
-LAST_LOADS = [(0, 512), (512, 1024), (1024, 1536), (1536, 1792), (1792, 2048)]
-LAST_CASTS = [(0, 512, "s"), (512, 1024, "s"), (1024, 1536, "v"), (1536, 1792, "s"), (1792, 2048, "v")]
+WHOLE = [(0, 2048)]
+HALVES = [(0, 1024), (1024, 2048)]
+LOADS = [HALVES, WHOLE, WHOLE, HALVES, HALVES, [(0, 1024), (1024, 1536), (1536, 2048)]]
+CASTS = [
+    [(0, 256, "g"), (256, 768, "s"), (768, 1024, "v"), (1024, 1280, "g"), (1280, 1728, "s"), (1728, 2048, "v")],
+    [(0, 448, "g"), (448, 1536, "s"), (1536, 2048, "v")],
+    [(0, 384, "g"), (384, 1792, "s"), (1792, 2048, "v")],
+    [(0, 256, "g"), (256, 1024, "s"), (1024, 1472, "g"), (1472, 2048, "s")],
+    [(0, 320, "g"), (320, 1024, "s"), (1024, 1280, "g"), (1280, 2048, "s")],
+    [(0, 384, "g"), (384, 1024, "s"), (1024, 1280, "g"), (1280, 1536, "s"), (1536, 1728, "g"), (1728, 2048, "s")],
+]
 
 
 def tile_picked_pool_lin_relu_sub_e_kernel(tc, xT, w_words, w_scales, b, offs, out):
@@ -38,17 +45,11 @@ def tile_picked_pool_lin_relu_sub_e_kernel(tc, xT, w_words, w_scales, b, offs, o
         result = keep.tile([P, V], F32, name="result")
         acc = [psum.tile([P, HALF], F32, name=f"acc{h}") for h in range(2)]
 
-        def loads(i):
-            return LAST_LOADS if i == 2 * PASSES - 1 else BODY_LOADS
-
-        def casts(i):
-            return LAST_CASTS if i == 2 * PASSES - 1 else BODY_CASTS
-
         nc.vector.memset(w_planes[:].rearrange("p a n -> p (a n)").bitcast(I32), 0)
         for i in range(2 * PASSES):
             a, u = divmod(i, 2)
             rows = xT[512 * a : 512 * (a + 1), :].rearrange("(p j) t -> p j t", j=4)
-            for t0, t1 in loads(i):
+            for t0, t1 in LOADS[i]:
                 nc.sync.dma_start(out=raw[i][:, :, t0:t1], in_=rows[:, 2 * u : 2 * u + 2, t0:t1])
             if i == 0:
                 nc.sync.dma_start(offsets[:], offs)
@@ -73,19 +74,7 @@ def tile_picked_pool_lin_relu_sub_e_kernel(tc, xT, w_words, w_scales, b, offs, o
                 in_=grouped[a][:].rearrange("p n j -> p (n j)")[:, 4 * c0 : 4 * c1],
             )
 
-        for i in range(2 * PASSES):
-            a, u = divmod(i, 2)
-            for t0, t1, engine in casts(i):
-                src = raw[i][:, :, t0:t1].rearrange("p e t -> p t e")
-                if engine == "s":
-                    nc.scalar.activation(pairs[i][:, t0:t1, :], src, Copy)
-                else:
-                    nc.vector.tensor_copy(out=pairs[i][:, t0:t1, :], in_=src)
-            if u == 0:
-                gather(i, 0, S)
-                continue
-            for h in range(2):
-                gather(i, h * HALF, (h + 1) * HALF)
+        def multiply(a):
             for h in range(2):
                 quantize(a, h * HALF, (h + 1) * HALF)
             for h in range(2):
@@ -99,6 +88,26 @@ def tile_picked_pool_lin_relu_sub_e_kernel(tc, xT, w_words, w_scales, b, offs, o
                     start=(a == 0),
                     stop=(a == PASSES - 1),
                 )
+
+        for i in range(2 * PASSES):
+            a, u = divmod(i, 2)
+            for t0, t1, engine in CASTS[i]:
+                src = raw[i][:, :, t0:t1].rearrange("p e t -> p t e")
+                if engine == "s":
+                    nc.scalar.activation(pairs[i][:, t0:t1, :], src, Copy)
+                elif engine == "g":
+                    nc.gpsimd.tensor_copy(out=pairs[i][:, t0:t1, :], in_=src)
+                else:
+                    nc.vector.tensor_copy(out=pairs[i][:, t0:t1, :], in_=src)
+            if i == 2:
+                multiply(0)
+            if u == 0:
+                gather(i, 0, S)
+            else:
+                gather(i, 0, HALF)
+                gather(i, HALF, S)
+            if i > 1 and u == 1:
+                multiply(a)
         for h in range(2):
             nc.vector.tensor_reduce(
                 out=largest[:, h * V // 2 : (h + 1) * V // 2],

import concourse.mybir as mybir

K, T, D, S, V, N = 1536, 2048, 16, 1024, 64, 128
FLOPS = 2 * K * S * N

F32 = mybir.dt.float32
BF16 = mybir.dt.bfloat16
I32 = mybir.dt.int32
U32 = mybir.dt.uint32
U16 = mybir.dt.uint16
U8 = mybir.dt.uint8
FP8X4 = mybir.dt.float8_e4m3fn_x4
Copy = mybir.ActivationFunctionType.Copy
Op = mybir.AluOpType

P = 128
PASSES = K // 512
HALF = S // 2
WHOLE = [(0, 2048)]
HALVES = [(0, 1024), (1024, 2048)]
LOADS = [HALVES, WHOLE, WHOLE, HALVES, HALVES, [(0, 1024), (1024, 1536), (1536, 2048)]]
CASTS = [
    [(0, 256, "g"), (256, 768, "s"), (768, 1024, "v"), (1024, 1280, "g"), (1280, 1728, "s"), (1728, 2048, "v")],
    [(0, 448, "g"), (448, 1536, "s"), (1536, 2048, "v")],
    [(0, 384, "g"), (384, 1792, "s"), (1792, 2048, "v")],
    [(0, 256, "g"), (256, 1024, "s"), (1024, 1472, "g"), (1472, 2048, "s")],
    [(0, 320, "g"), (320, 1024, "s"), (1024, 1280, "g"), (1280, 2048, "s")],
    [(0, 384, "g"), (384, 1024, "s"), (1024, 1280, "g"), (1280, 1536, "s"), (1536, 1728, "g"), (1728, 2048, "s")],
]


def tile_picked_pool_lin_relu_sub_e_kernel(tc, xT, w_words, w_scales, b, offs, out):
    nc = tc.nc
    with tc.tile_pool(name="keep", bufs=1) as keep, tc.psum_pool(name="psum", bufs=1) as psum:
        offsets = keep.tile([P, S // 16], U16, name="offsets")
        w_codes = keep.tile([P, PASSES, N * 4], U8, name="w_codes", align_bytes=64)
        w_planes = keep.tile([P, PASSES, N], U8, name="w_planes", align_bytes=64)
        bias = keep.tile([P, 1], F32, name="bias")
        raw = [keep.tile([P, 2, T], F32, name=f"raw{i}") for i in range(2 * PASSES)]
        pairs = [keep.tile([P, T, 2], BF16, name=f"pairs{i}", align_bytes=64) for i in range(2 * PASSES)]
        grouped = [keep.tile([P, S, 4], BF16, name=f"grouped{a}", align_bytes=64) for a in range(PASSES)]
        codes = [keep.tile([P, S], U32, name=f"codes{a}", align_bytes=64) for a in range(PASSES)]
        planes = [keep.tile([P, S], U8, name=f"planes{a}", align_bytes=64) for a in range(PASSES)]
        largest = keep.tile([P, V], F32, name="largest")
        result = keep.tile([P, V], F32, name="result")
        acc = [psum.tile([P, HALF], F32, name=f"acc{h}") for h in range(2)]

        nc.vector.memset(w_planes[:].rearrange("p a n -> p (a n)").bitcast(I32), 0)
        for i in range(2 * PASSES):
            a, u = divmod(i, 2)
            rows = xT[512 * a : 512 * (a + 1), :].rearrange("(p j) t -> p j t", j=4)
            for t0, t1 in LOADS[i]:
                nc.sync.dma_start(out=raw[i][:, :, t0:t1], in_=rows[:, 2 * u : 2 * u + 2, t0:t1])
            if i == 0:
                nc.sync.dma_start(offsets[:], offs)
                nc.scalar.dma_start(out=w_codes[:].bitcast(I32), in_=w_words.rearrange("a p m r -> p a (m r)").bitcast(I32))
                for q in range(4):
                    nc.scalar.dma_start(
                        out=w_planes[32 * q : 32 * q + 4, :, :].bitcast(I32),
                        in_=w_scales[:, 4 * q : 4 * q + 4, :].rearrange("a q m -> q a m").bitcast(I32),
                    )
                nc.scalar.dma_start(out=bias[:], in_=b)

        def gather(i, c0, c1):
            a, u = divmod(i, 2)
            words = grouped[a][:].rearrange("p n j -> p (n j)").bitcast(U32).rearrange("p (n u) -> p n u", u=2)
            window = pairs[i][:].rearrange("p t e -> p (t e)").bitcast(U32)
            nc.vector.tensor_copy(out=words[:, c0:c1, u], in_=window.indirect(offsets[:, c0 // 16 : c1 // 16]))

        def quantize(a, c0, c1):
            nc.vector.quantize_mx(
                out=codes[a][:, c0:c1].bitcast(FP8X4),
                scales=planes[a][:, c0:c1],
                in_=grouped[a][:].rearrange("p n j -> p (n j)")[:, 4 * c0 : 4 * c1],
            )

        def multiply(a):
            for h in range(2):
                quantize(a, h * HALF, (h + 1) * HALF)
            for h in range(2):
                cols = slice(h * HALF, (h + 1) * HALF)
                nc.tensor.matmul_mx(
                    out=acc[h][:],
                    lhsT=w_codes[:, a, :].bitcast(FP8X4),
                    lhsT_scale=w_planes[:, a, :],
                    rhs=codes[a][:, cols].bitcast(FP8X4),
                    rhs_scale=planes[a][:, cols],
                    start=(a == 0),
                    stop=(a == PASSES - 1),
                )

        for i in range(2 * PASSES):
            a, u = divmod(i, 2)
            for t0, t1, engine in CASTS[i]:
                src = raw[i][:, :, t0:t1].rearrange("p e t -> p t e")
                if engine == "s":
                    nc.scalar.activation(pairs[i][:, t0:t1, :], src, Copy)
                elif engine == "g":
                    nc.gpsimd.tensor_copy(out=pairs[i][:, t0:t1, :], in_=src)
                else:
                    nc.vector.tensor_copy(out=pairs[i][:, t0:t1, :], in_=src)
            if i == 2:
                multiply(0)
            if u == 0:
                gather(i, 0, S)
            else:
                gather(i, 0, HALF)
                gather(i, HALF, S)
            if i > 1 and u == 1:
                multiply(a)
        for h in range(2):
            nc.vector.tensor_reduce(
                out=largest[:, h * V // 2 : (h + 1) * V // 2],
                in_=acc[h][:].rearrange("p (v d) -> p v d", d=D),
                axis=mybir.AxisListType.X,
                op=Op.max,
            )
        nc.vector.tensor_scalar(out=result[:], in0=largest[:], scalar1=bias[:, 0:1], scalar2=0.0, op0=Op.add, op1=Op.max)
        nc.sync.dma_start(out=out, in_=result[:])
